import numpy as np
import ml_dtypes


def mxq(x, axis, fmt="e4m3"):
    dtype, down = {"e4m3": (ml_dtypes.float8_e4m3fn, 7), "e5m2": (ml_dtypes.float8_e5m2, 14)}[fmt]
    v = np.moveaxis(np.asarray(x, np.float32).astype(ml_dtypes.bfloat16).astype(np.float64), axis, -1)
    blocks = v.reshape(v.shape[:-1] + (-1, 32))
    amax = np.abs(blocks).max(-1, keepdims=True)
    byte = np.maximum(np.where(amax > 0, np.frexp(amax)[1] - 1 + 127, 0) - down, 1)
    scale = np.exp2(byte - 127.0)
    codes = (blocks / scale).astype(np.float32).astype(dtype).astype(np.float64)
    return np.moveaxis((codes * scale).reshape(v.shape), -1, axis)


WIDE = False


def mx_kscale(k):
    if not WIDE:
        return np.ones(k)
    levels = np.array([10, -10, 5, -5, 0])
    if k % 512:
        return np.exp2(np.random.permutation(np.resize(levels, k // 32))).repeat(32)
    a = np.empty((k // 512, 16))
    for p in range(k // 512):
        a[p, :8] = np.random.permutation(np.resize(levels, 8))
        for g in range(8):
            far = levels[np.abs(levels - a[p, g]) >= 10]
            a[p, g + 8] = far[np.random.randint(len(far))]
    return np.exp2(a.ravel()).repeat(32)


def f64(x):
    return np.asarray(x).astype(np.float64)


def striped(idx):
    return np.tile(idx.reshape(-1, 16).T, (8, 1)).astype(np.uint16)


def unstriped(offs):
    return offs[:16].T.reshape(-1).astype(np.int64)


E2M1 = np.array([0.0, 0.5, 1.0, 1.5, 2.0, 3.0, 4.0, 6.0, -0.0, -0.5, -1.0, -1.5, -2.0, -3.0, -4.0, -6.0])


def pack_weight(w, fmt):
    k, n = w.shape
    w = f64(np.asarray(w, np.float32).astype(ml_dtypes.bfloat16)).reshape(k // 32, 32, n)
    amax = np.abs(w).max(1)
    if fmt == "e4m3":
        byte = np.frexp(amax)[1] - 1 + 127 - 7
    else:
        mant, ex = np.frexp(amax / 6.0)
        byte = np.where(mant > 0.5, ex, ex - 1) + 127
    byte = np.clip(np.where(amax > 0, byte, 1), 1, 254)
    scaled = (w * np.exp2(127.0 - byte)[:, None, :]).reshape(k, n).astype(np.float32)
    by_word = np.ascontiguousarray(scaled.reshape(k // 512, 128, 4, n).transpose(0, 1, 3, 2))
    if fmt == "e4m3":
        words = by_word.astype(ml_dtypes.float8_e4m3fn).view(np.uint8)
    else:
        c = by_word.astype(ml_dtypes.float4_e2m1fn).view(np.uint8) & 0xF
        words = (c[..., 0::2] | (c[..., 1::2] << 4)).reshape(k // 512, 128, 2 * n)
    return np.ascontiguousarray(words), np.ascontiguousarray(byte.astype(np.uint8).reshape(k // 512, 16, n))


def unpack_weight(words, scales, fmt):
    g, _, n = scales.shape
    words = np.ascontiguousarray(words).reshape(g, 128, n, -1)
    if fmt == "e4m3":
        vals = words.view(ml_dtypes.float8_e4m3fn).astype(np.float64)
    else:
        nib = np.empty((g, 128, n, 4), np.uint8)
        nib[..., 0::2] = words & 0xF
        nib[..., 1::2] = words >> 4
        vals = E2M1[nib]
    vals = vals * np.repeat(np.exp2(scales.astype(np.float64) - 127.0), 8, axis=1)[..., None]
    return vals.transpose(0, 1, 3, 2).reshape(g * 512, n)


def gelu(v):
    return 0.5 * v * (1.0 + np.tanh(np.sqrt(2.0 / np.pi) * (v + 0.044715 * v**3)))


def striped8(idx):
    return np.concatenate([v.reshape(-1, 16).T for v in idx]).astype(np.uint16)


def unstriped8(offs):
    return np.stack([offs[16 * g:16 * g + 16].T.reshape(-1) for g in range(8)]).astype(np.int64)


def heads(h, wgt, idx8):
    r = np.arange(h.shape[0])
    return wgt[r // 4 % 128] * h[r[:, None], idx8[r % 512 // 64]]


K, T, S, H, P, N = 1024, 4096, 1024, 1024, 512, 512

def setup_inputs():
    n = np.random.standard_normal
    s = mx_kscale(K)[:, None]
    u = mx_kscale(H)[:, None]
    tab_words, tab_scales = pack_weight(n((K, T)) * s, "e4m3")
    w1 = (n((K, H)) / np.sqrt(K) / s * u.T).astype(np.float32)
    w2_words, w2_scales = pack_weight(n((K, H)) / np.sqrt(K) / s * u.T, "e2m1")
    w3 = (0.6 * n((H, N)) / np.sqrt(H) / u).astype(np.float32)
    w4_words, w4_scales = pack_weight(0.6 * n((H, N)) / np.sqrt(H) / u, "e4m3")
    return {
        "tab_words": tab_words, "tab_scales": tab_scales,
        "offs": striped(np.random.permutation(T)[:S]),
        "offs2": striped8(np.stack([np.random.permutation(S)[:P] for _ in range(8)])),
        "offs3": striped8(np.stack([np.random.permutation(S)[:P] for _ in range(8)])),
        "w1": w1, "w2_words": w2_words, "w2_scales": w2_scales,
        "ba": (0.6 * n(H) * u[:, 0]).astype(np.float32),
        "bb": (0.6 * n(H) * u[:, 0]).astype(np.float32),
        "wga": np.repeat(np.random.uniform(0.5, 2.0, (8, P)), 16, axis=0).astype(np.float32),
        "wgb": np.repeat(np.random.uniform(0.5, 2.0, (8, P)), 16, axis=0).astype(np.float32),
        "w3": w3, "w4_words": w4_words, "w4_scales": w4_scales,
        "by": (0.6 * n(N)).astype(np.float32),
        "cov": np.random.uniform(0.4, 1.6, P).astype(np.float32),
    }

def reference(tab_words, tab_scales, offs, offs2, offs3, w1, w2_words, w2_scales, ba, bb, wga, wgb, w3, w4_words, w4_scales, by, cov):
    v = unpack_weight(tab_words, tab_scales, "e4m3")[:, unstriped(offs)]
    w2 = unpack_weight(w2_words, w2_scales, "e2m1")
    w4 = unpack_weight(w4_words, w4_scales, "e4m3")
    ha = (mxq(f64(w1), 0, "e4m3").T @ v) + f64(ba)[:, None]
    hb = (w2.T @ v) + f64(bb)[:, None]
    xa = heads(ha, f64(wga), unstriped8(offs2))
    xb = heads(hb, f64(wgb), unstriped8(offs3))
    hi = mxq(np.maximum(xa, xb), 0, "e4m3")
    lo = mxq(np.minimum(xa, xb), 0, "e4m3")
    y = mxq(f64(w3), 0, "e4m3").T @ hi + w4.T @ lo
    return np.tanh(y + f64(by)[:, None]) * f64(cov)[None, :]

@@ -1,0 +1,303 @@
+from contextlib import ExitStack
+
+import concourse.mybir as mybir
+
+K, T, S, H, M, N = 1024, 4096, 1024, 1024, 512, 512
+FLOPS = 2 * (2 * K * H * S + 2 * H * N * M)
+
+F32 = mybir.dt.float32
+BF16 = mybir.dt.bfloat16
+I32 = mybir.dt.int32
+U32 = mybir.dt.uint32
+U16 = mybir.dt.uint16
+U8 = mybir.dt.uint8
+FP8X4 = mybir.dt.float8_e4m3fn_x4
+FP4X4 = mybir.dt.float4_e2m1fn_x4
+ALU = mybir.AluOpType
+ACT = mybir.ActivationFunctionType
+
+P = 128
+PACK = 4
+PASS = P * PACK
+BANK = 512
+HALF = 256
+
+
+def tile_list_burial_kin_scores_kernel(
+    tc, tab_words, tab_scales, offs, offs2, offs3, w1, w2_words, w2_scales, ba, bb,
+    wga, wgb, w3, w4_words, w4_scales, by, cov, out,
+):
+    nc = tc.nc
+    with ExitStack() as ctx:
+        lists = ctx.enter_context(tc.tile_pool(name="lists", bufs=1))
+        keep = ctx.enter_context(tc.tile_pool(name="keep", bufs=1))
+        ring = ctx.enter_context(tc.tile_pool(name="ring", bufs=4))
+        hpool = ctx.enter_context(tc.tile_pool(name="hpool", bufs=6))
+        h_psum = ctx.enter_context(tc.psum_pool(name="h_psum", bufs=4))
+        y_psum = ctx.enter_context(tc.psum_pool(name="y_psum", bufs=1))
+
+        def held(shape, dtype, name, tag=None):
+            return keep.tile(shape, dtype, name=name, tag=tag or name, align_bytes=64)
+
+        idx = lists.tile([P, S // 16], U16, name="idx")
+        idx_a = lists.tile([P, M // 16], U16, name="idx_a")
+        idx_b = lists.tile([P, M // 16], U16, name="idx_b")
+
+        shared = ctx.enter_context(tc.tile_pool(name="shared", bufs=1))
+        scale_rows = shared.tile([P, T], U8, name="scale_rows", offset=2048, align_bytes=64)
+        w2_scale_raw = held([P, 2, H], U8, "w2_scale_raw")
+        v_scale = [held([P, S], U8, "v_scale%d" % a) for a in range(2)]
+        nc.vector.memset(scale_rows[:].bitcast(I32), 0)
+        nc.vector.memset(w2_scale_raw[:].bitcast(I32), 0)
+        for a in range(2):
+            nc.vector.memset(v_scale[a][:].bitcast(I32), 0)
+
+        nc.sync.dma_start(idx[:], offs)
+        w2_raw = held([P, 2, 2 * H], U8, "w2_raw")
+        nc.sync.dma_start(w2_raw[:].bitcast(I32), w2_words.rearrange("a p c -> p a c").bitcast(I32))
+        nc.sync.dma_start(idx_b[:], offs3)
+        nc.sync.dma_start(idx_a[:], offs2)
+
+        def load_table(words, a):
+            nc.sync.dma_start(
+                words[:].bitcast(I32), tab_words[a].rearrange("p t i -> p (t i)").bitcast(I32)
+            )
+
+        table0 = held([P, T], U32, "table0")
+        load_table(table0, 0)
+        nc.scalar.dma_start(
+            scale_rows[0:P:4, :].bitcast(I32), tab_scales.rearrange("a q t -> (a q) t").bitcast(I32)
+        )
+
+        def load_scale_rows(queue, plane, dram):
+            for quad in range(4):
+                queue.dma_start(
+                    plane[32 * quad : 32 * quad + 4, :, :].bitcast(I32),
+                    dram[:, 4 * quad : 4 * quad + 4, :].rearrange("a r c -> r a c").bitcast(I32),
+                )
+
+        load_scale_rows(nc.scalar, w2_scale_raw, w2_scales)
+
+        with tc.tile_pool(name="early", bufs=1) as early:
+            picked_rows = early.tile([P, S], U8, name="picked_rows")
+            nc.vector.tensor_copy(picked_rows[:], scale_rows[:].indirect(idx[:]))
+            table1 = shared.tile([P, T], U32, name="table1", offset=4096, align_bytes=64)
+            load_table(table1, 1)
+            for a in range(2):
+                for quad in range(4):
+                    first = 64 * a + 16 * quad
+                    nc.scalar.dma_start(
+                        v_scale[a][32 * quad : 32 * quad + 4, :].bitcast(I32),
+                        picked_rows[first : first + 16 : 4, :].bitcast(I32),
+                    )
+
+        late = ctx.enter_context(tc.tile_pool(name="late", bufs=1))
+
+        def load_rows(dram, a, cols):
+            raw = late.tile([P, PACK, BANK], F32, name="raw", bufs=4)
+            nc.sync.dma_start(
+                raw[:], dram[PASS * a : PASS * (a + 1), cols].rearrange("(p j) c -> p j c", j=PACK)
+            )
+            return raw
+
+        bias_b = late.tile([P, 2, PACK], F32, name="bias_b")
+        nc.sync.dma_start(bias_b[:], bb.rearrange("(b p t) -> p b t", b=2, t=PACK))
+        weight_b = late.tile([P, M], F32, name="weight_b")
+        nc.sync.dma_start(weight_b[:], wgb)
+        w1_raw = {}
+        for a in range(2):
+            w1_raw[a, 0] = load_rows(w1, a, slice(0, BANK))
+        bias_a = late.tile([P, 2, PACK], F32, name="bias_a")
+        nc.sync.dma_start(bias_a[:], ba.rearrange("(b p t) -> p b t", b=2, t=PACK))
+        weight_a = late.tile([P, M], F32, name="weight_a")
+        nc.sync.dma_start(weight_a[:], wga)
+        for a in range(2):
+            w1_raw[a, 1] = load_rows(w1, a, slice(BANK, 2 * BANK))
+
+        w2_code = held([P, 2 * 2 * H], U8, "w2_code")
+        nc.vector.tensor_copy(
+            w2_code[:].bitcast(U16).rearrange("p (g t m) -> p g t m", t=PACK, m=P),
+            w2_raw[:].rearrange("p a c -> p (a c)").bitcast(U16).rearrange("p (g m t) -> p g t m", t=PACK, m=P),
+        )
+        v_code0 = shared.tile([P, S], U32, name="v_code0", offset=0, align_bytes=64)
+        nc.vector.tensor_copy(v_code0[:], table0[:].indirect(idx[:]))
+        v_code = {(0, half): v_code0[:, BANK * half : BANK * (half + 1)] for half in range(2)}
+        w2_scale = held([P, 2 * H], U8, "w2_scale")
+        nc.vector.tensor_copy(
+            w2_scale[:].rearrange("p (g t m) -> p g t m", t=PACK, m=P),
+            w2_scale_raw[:].rearrange("p a (b m t) -> p (a b) t m", t=PACK, m=P),
+        )
+        for half in range(2):
+            picked = held([P, BANK], U32, "v_code1%d" % half, None if half else "w2_scale_raw")
+            nc.vector.tensor_copy(picked[:], table1[:].indirect(idx[:, 32 * half : 32 * (half + 1)]))
+            v_code[1, half] = picked[:]
+
+        def copy_on(engine, dst, src):
+            if engine == "scalar":
+                nc.scalar.copy(dst, src)
+            else:
+                nc.vector.tensor_copy(dst, src)
+
+        def quantize(grouped, name, width=BANK):
+            code = held([P, width], U32, name + "_code")
+            scale = held([P, width], U8, name + "_scale")
+            nc.vector.quantize_mx(out=code[:].bitcast(FP8X4), scales=scale[:], in_=grouped[:])
+            return code, scale
+
+        w1_grouped = {}
+        w1_mx = {}
+
+        def round_w1(a, b, pair, engine):
+            if (a, b) not in w1_grouped:
+                w1_grouped[a, b] = ring.tile([P, PACK * BANK], BF16, name="grouped", align_bytes=64)
+            ts = slice(2 * pair, 2 * pair + 2)
+            copy_on(
+                engine,
+                w1_grouped[a, b][:].rearrange("p (t m j) -> p m j t", t=PACK, j=PACK)[:, :, :, ts],
+                w1_raw[a, b][:].rearrange("p j (m t) -> p m j t", t=PACK)[:, :, :, ts],
+            )
+
+        def quantize_w1(a, b):
+            w1_mx[a, b] = quantize(w1_grouped[a, b], "w1_%d%d" % (a, b))
+
+        def w1_operand(a, b, t):
+            code, scale = w1_mx[a, b]
+            return code[:, P * t : P * (t + 1)].bitcast(FP8X4), scale[:, P * t : P * (t + 1)]
+
+        def w2_operand(a, b, t):
+            col = H * a + BANK * b + P * t
+            return w2_code[:, 2 * col : 2 * (col + P)].bitcast(FP4X4), w2_scale[:, col : col + P]
+
+        def h_slice(operand, bias, b, t):
+            h = hpool.tile([P, S], F32, name="h")
+            for half in range(2):
+                cols = slice(BANK * half, BANK * (half + 1))
+                acc = h_psum.tile([P, BANK], F32, name="acc")
+                for a in range(2):
+                    code, scale = operand(a, b, t)
+                    nc.tensor.matmul_mx(
+                        out=acc[:], lhsT=code, lhsT_scale=scale,
+                        rhs=v_code[a, half].bitcast(FP8X4), rhs_scale=v_scale[a][:, cols],
+                        start=(a == 0), stop=(a == 1),
+                    )
+                nc.scalar.activation(h[:, cols], acc[:], ACT.Identity, bias=bias[:, b, t : t + 1])
+            return h
+
+        xa0 = held([P, PACK, M], F32, "xa0")
+        xb = [held([P, PACK, M], F32, "xb%d" % b) for b in range(2)]
+
+
+        def pick_b(b, t):
+            h = h_slice(w2_operand, bias_b, b, t)
+            nc.vector.tensor_tensor(xb[b][:, t, :], h[:].indirect(idx_b[:]), weight_b[:], ALU.mult)
+
+        def extreme(left, right, op, width):
+            grouped = ring.tile([P, PACK * width], BF16, name="grouped", align_bytes=64)
+            nc.vector.tensor_tensor(
+                grouped[:].rearrange("p (c i t) -> p c t i", i=2, t=PACK),
+                left.rearrange("p t (c i) -> p c t i", i=2),
+                right.rearrange("p t (c i) -> p c t i", i=2),
+                op,
+            )
+            return grouped
+
+        def extremes(left, right, name, width):
+            hi_grouped = extreme(left, right, ALU.max, width)
+            lo_grouped = extreme(left, right, ALU.min, width)
+            return quantize(hi_grouped, "hi" + name, width), quantize(lo_grouped, "lo" + name, width)
+
+        pick_b(0, 0)
+        round_w1(0, 0, 0, "vector")
+        round_w1(0, 0, 1, "scalar")
+        pick_b(0, 1)
+        quantize_w1(0, 0)
+        pick_b(0, 2)
+        round_w1(1, 0, 0, "vector")
+        round_w1(1, 0, 1, "scalar")
+        pick_b(0, 3)
+        quantize_w1(1, 0)
+
+        w3_raw = [load_rows(w3, a, slice(0, N)) for a in range(2)]
+        w4_code = late.tile([P, 2, N], U32, name="w4_code", align_bytes=64)
+        w4_scale = late.tile([P, 2, N], U8, name="w4_scale", align_bytes=64)
+        nc.vector.memset(w4_scale[:].bitcast(I32), 0)
+        nc.sync.dma_start(
+            w4_code[:].bitcast(I32), w4_words.rearrange("a p c i -> p a (c i)").bitcast(I32)
+        )
+        load_scale_rows(nc.sync, w4_scale, w4_scales)
+        bias_y = late.tile([P, N // P], F32, name="bias_y")
+        with nc.allow_non_contiguous_dma(reason="one bias value for each output row"):
+            nc.sync.dma_start(bias_y[:], by.rearrange("(s p) -> p s", p=P))
+        cover = late.tile([P, M], F32, name="cover")
+        nc.sync.dma_start(cover[:], cov.partition_broadcast(P))
+
+        for t in range(PACK):
+            h = h_slice(w1_operand, bias_a, 0, t)
+            nc.vector.tensor_tensor(xa0[:, t, :], h[:].indirect(idx_a[:]), weight_a[:], ALU.mult)
+            round_w1(t // 2, 1, t % 2, "scalar")
+            if t % 2:
+                quantize_w1(t // 2, 1)
+
+        hi0, lo0 = extremes(xa0[:], xb[0][:], "0", M)
+        for t in range(PACK):
+            pick_b(1, t)
+
+        def round_w3(a):
+            grouped = ring.tile([P, PACK * BANK], BF16, name="grouped", align_bytes=64)
+            nc.scalar.copy(
+                grouped[:].rearrange("p (c i j) -> p c j i", i=2, j=PACK),
+                w3_raw[a][:].rearrange("p j (c i) -> p c j i", i=2),
+            )
+            return quantize(grouped, "w3_%d" % a)
+
+        def pick_half(h, xa1, t, half):
+            nc.vector.tensor_tensor(
+                xa1[:, t, :], h[:].indirect(idx_a[:, 16 * half : 16 * (half + 1)]),
+                weight_a[:, HALF * half : HALF * (half + 1)], ALU.mult,
+            )
+
+        ha1, w3_mx = [], []
+        xa1 = held([P, PACK, HALF], F32, "xa10", "xa1")
+        for t in range(PACK):
+            ha1.append(h_slice(w1_operand, bias_a, 1, t))
+            pick_half(ha1[t], xa1, t, 0)
+            if t % 2:
+                w3_mx.append(round_w3(t // 2))
+
+        def y_passes(y, weight, operand, cols, first, last):
+            for s in range(N // P):
+                rows = slice(P * s, P * (s + 1))
+                nc.tensor.matmul_mx(
+                    out=y[s // 2][:, s % 2, :], lhsT=weight[0][:, rows].bitcast(FP8X4),
+                    lhsT_scale=weight[1][:, rows], rhs=operand[0][:, cols].bitcast(FP8X4),
+                    rhs_scale=operand[1][:, cols],
+                    start=(first and s % 2 == 0), stop=(last and s % 2 == 1),
+                )
+
+        w4_mx = [(w4_code[:, b, :], w4_scale[:, b, :]) for b in range(2)]
+        for half in range(2):
+            cols = slice(HALF * half, HALF * (half + 1))
+            if half:
+                xa1 = held([P, PACK, HALF], F32, "xa11", "xa1")
+                for t in range(PACK):
+                    pick_half(ha1[t], xa1, t, 1)
+            hi1, lo1 = extremes(xa1[:], xb[1][:, :, cols], "1%d" % half, HALF)
+            y = [y_psum.tile([P, 2, HALF], F32, name="y%d%d" % (half, pair)) for pair in range(2)]
+            y_passes(y, w3_mx[0], hi0, cols, True, False)
+            y_passes(y, w4_mx[0], lo0, cols, False, False)
+            y_passes(y, w3_mx[1], hi1, slice(0, HALF), False, False)
+            y_passes(y, w4_mx[1], lo1, slice(0, HALF), False, True)
+            for pair in range(2):
+                bounded = held([P, 2, HALF], F32, "bounded%d%d" % (half, pair))
+                for k in range(2):
+                    s = 2 * pair + k
+                    nc.scalar.activation(
+                        bounded[:, k, :], y[pair][:, k, :], ACT.Tanh, bias=bias_y[:, s : s + 1]
+                    )
+                score = held([P, 2, HALF], F32, "score%d%d" % (half, pair))
+                nc.vector.tensor_tensor(
+                    score[:], bounded[:], cover[:, cols].unsqueeze(1).to_broadcast([P, 2, HALF]), ALU.mult
+                )
+                nc.sync.dma_start(
+                    out[2 * P * pair : 2 * P * (pair + 1), cols].rearrange("(k p) m -> p k m", p=P), score[:]
+                )

@@ -20,7 +20,8 @@ P = 128
 PACK = 4
 PASS = P * PACK
 BANK = 512
-HALF = 256
+LAST = 128
+FIRST = M - LAST
 
 
 def tile_list_burial_kin_scores_kernel(
@@ -33,8 +34,7 @@ def tile_list_burial_kin_scores_kernel(
         keep = ctx.enter_context(tc.tile_pool(name="keep", bufs=1))
         ring = ctx.enter_context(tc.tile_pool(name="ring", bufs=4))
         hpool = ctx.enter_context(tc.tile_pool(name="hpool", bufs=6))
-        h_psum = ctx.enter_context(tc.psum_pool(name="h_psum", bufs=4))
-        y_psum = ctx.enter_context(tc.psum_pool(name="y_psum", bufs=1))
+        psum = ctx.enter_context(tc.psum_pool(name="psum", bufs=8))
 
         def held(shape, dtype, name, tag=None):
             return keep.tile(shape, dtype, name=name, tag=tag or name, align_bytes=64)
@@ -43,55 +43,58 @@ def tile_list_burial_kin_scores_kernel(
         idx_a = lists.tile([P, M // 16], U16, name="idx_a")
         idx_b = lists.tile([P, M // 16], U16, name="idx_b")
 
-        shared = ctx.enter_context(tc.tile_pool(name="shared", bufs=1))
-        scale_rows = shared.tile([P, T], U8, name="scale_rows", offset=2048, align_bytes=64)
-        w2_scale_raw = held([P, 2, H], U8, "w2_scale_raw")
-        v_scale = [held([P, S], U8, "v_scale%d" % a) for a in range(2)]
-        nc.vector.memset(scale_rows[:].bitcast(I32), 0)
-        nc.vector.memset(w2_scale_raw[:].bitcast(I32), 0)
-        for a in range(2):
-            nc.vector.memset(v_scale[a][:].bitcast(I32), 0)
-
-        nc.sync.dma_start(idx[:], offs)
-        w2_raw = held([P, 2, 2 * H], U8, "w2_raw")
-        nc.sync.dma_start(w2_raw[:].bitcast(I32), w2_words.rearrange("a p c -> p a c").bitcast(I32))
-        nc.sync.dma_start(idx_b[:], offs3)
-        nc.sync.dma_start(idx_a[:], offs2)
+        def load_scale_rows(plane, dram):
+            for quad in range(4):
+                nc.sync.dma_start(
+                    plane[32 * quad : 32 * quad + 4, :, :].bitcast(I32),
+                    dram[:, 4 * quad : 4 * quad + 4, :].rearrange("a r c -> r a c").bitcast(I32),
+                )
 
         def load_table(words, a):
             nc.sync.dma_start(
                 words[:].bitcast(I32), tab_words[a].rearrange("p t i -> p (t i)").bitcast(I32)
             )
 
-        table0 = held([P, T], U32, "table0")
-        load_table(table0, 0)
-        nc.scalar.dma_start(
-            scale_rows[0:P:4, :].bitcast(I32), tab_scales.rearrange("a q t -> (a q) t").bitcast(I32)
-        )
-
-        def load_scale_rows(queue, plane, dram):
-            for quad in range(4):
-                queue.dma_start(
-                    plane[32 * quad : 32 * quad + 4, :, :].bitcast(I32),
-                    dram[:, 4 * quad : 4 * quad + 4, :].rearrange("a r c -> r a c").bitcast(I32),
-                )
-
-        load_scale_rows(nc.scalar, w2_scale_raw, w2_scales)
-
+        picked_rows = held([P, S], U8, "picked_rows")
         with tc.tile_pool(name="early", bufs=1) as early:
-            picked_rows = early.tile([P, S], U8, name="picked_rows")
-            nc.vector.tensor_copy(picked_rows[:], scale_rows[:].indirect(idx[:]))
-            table1 = shared.tile([P, T], U32, name="table1", offset=4096, align_bytes=64)
-            load_table(table1, 1)
+            scale_rows = early.tile([P, T], U8, name="scale_rows")
+            w2_scale_raw = held([P, 2, H], U8, "w2_scale_raw")
+            v_scale = [held([P, S], U8, "v_scale%d" % a) for a in range(2)]
+            nc.vector.memset(scale_rows[:].bitcast(I32), 0)
+            nc.vector.memset(w2_scale_raw[:].bitcast(I32), 0)
             for a in range(2):
-                for quad in range(4):
-                    first = 64 * a + 16 * quad
-                    nc.scalar.dma_start(
-                        v_scale[a][32 * quad : 32 * quad + 4, :].bitcast(I32),
-                        picked_rows[first : first + 16 : 4, :].bitcast(I32),
-                    )
+                nc.vector.memset(v_scale[a][:].bitcast(I32), 0)
+
+            nc.sync.dma_start(idx[:], offs)
+            w2_raw = held([P, 2, 2 * H], U8, "w2_raw")
+            nc.sync.dma_start(w2_raw[:].bitcast(I32), w2_words.rearrange("a p c -> p a c").bitcast(I32))
+            nc.sync.dma_start(
+                scale_rows[0:P:4, :].bitcast(I32), tab_scales.rearrange("a q t -> (a q) t").bitcast(I32)
+            )
+            load_scale_rows(w2_scale_raw, w2_scales)
+            nc.sync.dma_start(idx_b[:], offs3)
+            nc.sync.dma_start(idx_a[:], offs2)
+            bias_b = held([P, 2, PACK], F32, "bias_b")
+            nc.sync.dma_start(bias_b[:], bb.rearrange("(b p t) -> p b t", b=2, t=PACK))
+            table0 = held([P, T], U32, "table0")
+            load_table(table0, 0)
+            nc.vector.tensor_copy(picked_rows[:], scale_rows[:].indirect(idx[:]))
 
         late = ctx.enter_context(tc.tile_pool(name="late", bufs=1))
+
+        def move_scale_rows(a, quad):
+            first = 64 * a + 16 * quad
+            nc.sync.dma_start(
+                v_scale[a][32 * quad : 32 * quad + 4, :].bitcast(I32),
+                picked_rows[first : first + 16 : 4, :].bitcast(I32),
+            )
+
+        for k in range(4):
+            move_scale_rows(k // 4, k % 4)
+        table1 = late.tile([P, T], U32, name="table1")
+        load_table(table1, 1)
+        for k in range(4, 8):
+            move_scale_rows(k // 4, k % 4)
 
         def load_rows(dram, a, cols):
             raw = late.tile([P, PACK, BANK], F32, name="raw", bufs=4)
@@ -100,8 +103,6 @@ def tile_list_burial_kin_scores_kernel(
             )
             return raw
 
-        bias_b = late.tile([P, 2, PACK], F32, name="bias_b")
-        nc.sync.dma_start(bias_b[:], bb.rearrange("(b p t) -> p b t", b=2, t=PACK))
         weight_b = late.tile([P, M], F32, name="weight_b")
         nc.sync.dma_start(weight_b[:], wgb)
         w1_raw = {}
@@ -114,12 +115,12 @@ def tile_list_burial_kin_scores_kernel(
         for a in range(2):
             w1_raw[a, 1] = load_rows(w1, a, slice(BANK, 2 * BANK))
 
-        w2_code = held([P, 2 * 2 * H], U8, "w2_code")
+        w2_code = late.tile([P, 2 * 2 * H], U8, name="w2_code", align_bytes=64)
         nc.vector.tensor_copy(
             w2_code[:].bitcast(U16).rearrange("p (g t m) -> p g t m", t=PACK, m=P),
             w2_raw[:].rearrange("p a c -> p (a c)").bitcast(U16).rearrange("p (g m t) -> p g t m", t=PACK, m=P),
         )
-        v_code0 = shared.tile([P, S], U32, name="v_code0", offset=0, align_bytes=64)
+        v_code0 = late.tile([P, S], U32, name="v_code0", align_bytes=64)
         nc.vector.tensor_copy(v_code0[:], table0[:].indirect(idx[:]))
         v_code = {(0, half): v_code0[:, BANK * half : BANK * (half + 1)] for half in range(2)}
         w2_scale = held([P, 2 * H], U8, "w2_scale")
@@ -172,7 +173,7 @@ def tile_list_burial_kin_scores_kernel(
             h = hpool.tile([P, S], F32, name="h")
             for half in range(2):
                 cols = slice(BANK * half, BANK * (half + 1))
-                acc = h_psum.tile([P, BANK], F32, name="acc")
+                acc = psum.tile([P, BANK], F32, name="acc")
                 for a in range(2):
                     code, scale = operand(a, b, t)
                     nc.tensor.matmul_mx(
@@ -212,7 +213,7 @@ def tile_list_burial_kin_scores_kernel(
         pick_b(0, 1)
         quantize_w1(0, 0)
         pick_b(0, 2)
-        round_w1(1, 0, 0, "vector")
+        round_w1(1, 0, 0, "scalar")
         round_w1(1, 0, 1, "scalar")
         pick_b(0, 3)
         quantize_w1(1, 0)
@@ -224,7 +225,7 @@ def tile_list_burial_kin_scores_kernel(
         nc.sync.dma_start(
             w4_code[:].bitcast(I32), w4_words.rearrange("a p c i -> p a (c i)").bitcast(I32)
         )
-        load_scale_rows(nc.sync, w4_scale, w4_scales)
+        load_scale_rows(w4_scale, w4_scales)
         bias_y = late.tile([P, N // P], F32, name="bias_y")
         with nc.allow_non_contiguous_dma(reason="one bias value for each output row"):
             nc.sync.dma_start(bias_y[:], by.rearrange("(s p) -> p s", p=P))
@@ -250,54 +251,71 @@ def tile_list_burial_kin_scores_kernel(
             )
             return quantize(grouped, "w3_%d" % a)
 
-        def pick_half(h, xa1, t, half):
+        def pick_part(h, xa1, t, cols):
             nc.vector.tensor_tensor(
-                xa1[:, t, :], h[:].indirect(idx_a[:, 16 * half : 16 * (half + 1)]),
-                weight_a[:, HALF * half : HALF * (half + 1)], ALU.mult,
+                xa1[:, t, :], h[:].indirect(idx_a[:, cols.start // 16 : cols.stop // 16]),
+                weight_a[:, cols], ALU.mult,
             )
 
+        first_cols, last_cols = slice(0, FIRST), slice(FIRST, M)
         ha1, w3_mx = [], []
-        xa1 = held([P, PACK, HALF], F32, "xa10", "xa1")
+        xa1 = held([P, PACK, FIRST], F32, "xa1_first", "xa1")
         for t in range(PACK):
             ha1.append(h_slice(w1_operand, bias_a, 1, t))
-            pick_half(ha1[t], xa1, t, 0)
+            pick_part(ha1[t], xa1, t, first_cols)
             if t % 2:
                 w3_mx.append(round_w3(t // 2))
-
-        def y_passes(y, weight, operand, cols, first, last):
-            for s in range(N // P):
-                rows = slice(P * s, P * (s + 1))
-                nc.tensor.matmul_mx(
-                    out=y[s // 2][:, s % 2, :], lhsT=weight[0][:, rows].bitcast(FP8X4),
-                    lhsT_scale=weight[1][:, rows], rhs=operand[0][:, cols].bitcast(FP8X4),
-                    rhs_scale=operand[1][:, cols],
-                    start=(first and s % 2 == 0), stop=(last and s % 2 == 1),
-                )
-
         w4_mx = [(w4_code[:, b, :], w4_scale[:, b, :]) for b in range(2)]
-        for half in range(2):
-            cols = slice(HALF * half, HALF * (half + 1))
-            if half:
-                xa1 = held([P, PACK, HALF], F32, "xa11", "xa1")
-                for t in range(PACK):
-                    pick_half(ha1[t], xa1, t, 1)
-            hi1, lo1 = extremes(xa1[:], xb[1][:, :, cols], "1%d" % half, HALF)
-            y = [y_psum.tile([P, 2, HALF], F32, name="y%d%d" % (half, pair)) for pair in range(2)]
-            y_passes(y, w3_mx[0], hi0, cols, True, False)
-            y_passes(y, w4_mx[0], lo0, cols, False, False)
-            y_passes(y, w3_mx[1], hi1, slice(0, HALF), False, False)
-            y_passes(y, w4_mx[1], lo1, slice(0, HALF), False, True)
-            for pair in range(2):
-                bounded = held([P, 2, HALF], F32, "bounded%d%d" % (half, pair))
-                for k in range(2):
-                    s = 2 * pair + k
-                    nc.scalar.activation(
-                        bounded[:, k, :], y[pair][:, k, :], ACT.Tanh, bias=bias_y[:, s : s + 1]
+
+        def y_pass(y, weight, s, operand, cols, start, stop):
+            rows = slice(P * s, P * (s + 1))
+            nc.tensor.matmul_mx(
+                out=y, lhsT=weight[0][:, rows].bitcast(FP8X4), lhsT_scale=weight[1][:, rows],
+                rhs=operand[0][:, cols].bitcast(FP8X4), rhs_scale=operand[1][:, cols],
+                start=start, stop=stop,
+            )
+
+        hi1, lo1 = extremes(xa1[:], xb[1][:, :, first_cols], "1_first", FIRST)
+        y_first = [psum.tile([P, FIRST], F32, name="y_first%d" % s, tag="acc") for s in range(N // P)]
+        products = [(w3_mx[0], hi0), (w4_mx[0], lo0), (w3_mx[1], hi1), (w4_mx[1], lo1)]
+        for k, (weight, operand) in enumerate(products):
+            for s in range(N // P):
+                for cols in (slice(0, 256), slice(256, FIRST)):
+                    y_pass(
+                        y_first[s][:, cols], weight, s, operand, cols,
+                        k == 0 and cols.start == 0, k == 3 and cols.stop == FIRST,
                     )
-                score = held([P, 2, HALF], F32, "score%d%d" % (half, pair))
-                nc.vector.tensor_tensor(
-                    score[:], bounded[:], cover[:, cols].unsqueeze(1).to_broadcast([P, 2, HALF]), ALU.mult
-                )
-                nc.sync.dma_start(
-                    out[2 * P * pair : 2 * P * (pair + 1), cols].rearrange("(k p) m -> p k m", p=P), score[:]
-                )
+        bounded_first = held([P, N // P, FIRST], F32, "bounded_first")
+        for s in range(N // P):
+            nc.scalar.activation(bounded_first[:, s, :], y_first[s][:], ACT.Tanh, bias=bias_y[:, s : s + 1])
+
+        xa1 = held([P, PACK, LAST], F32, "xa1_last", "xa1")
+        for t in range(PACK):
+            pick_part(ha1[t], xa1, t, last_cols)
+        hi1, lo1 = extremes(xa1[:], xb[1][:, :, last_cols], "1_last", LAST)
+        y_last = psum.tile([P, N // P, LAST], F32, name="y_last", tag="acc")
+        products = [
+            (w3_mx[0], hi0, last_cols), (w4_mx[0], lo0, last_cols),
+            (w3_mx[1], hi1, slice(0, LAST)), (w4_mx[1], lo1, slice(0, LAST)),
+        ]
+        for k, (weight, operand, cols) in enumerate(products):
+            for s in range(N // P):
+                y_pass(y_last[:, s, :], weight, s, operand, cols, k == 0 and s == 0, k == 3 and s == 3)
+        bounded_last = held([P, N // P, LAST], F32, "bounded_last")
+        for s in range(N // P):
+            nc.scalar.activation(bounded_last[:, s, :], y_last[:, s, :], ACT.Tanh, bias=bias_y[:, s : s + 1])
+
+        def store_scores(bounded, s0, count, cols, name):
+            width = cols.stop - cols.start
+            score = held([P, count, width], F32, name)
+            nc.vector.tensor_tensor(
+                score[:], bounded[:, s0 : s0 + count, :],
+                cover[:, cols].unsqueeze(1).to_broadcast([P, count, width]), ALU.mult,
+            )
+            nc.sync.dma_start(
+                out[P * s0 : P * (s0 + count), cols].rearrange("(k p) m -> p k m", p=P), score[:]
+            )
+
+        for pair in range(2):
+            store_scores(bounded_first, 2 * pair, 2, first_cols, "score_first%d" % pair)
+        store_scores(bounded_last, 0, N // P, last_cols, "score_last")

@@ -66,16 +66,16 @@ def tile_list_burial_kin_scores_kernel(
                 nc.vector.memset(v_scale[a][:].bitcast(I32), 0)
 
             nc.sync.dma_start(idx[:], offs)
-            w2_raw = held([P, 2, 2 * H], U8, "w2_raw")
-            nc.sync.dma_start(w2_raw[:].bitcast(I32), w2_words.rearrange("a p c -> p a c").bitcast(I32))
-            nc.sync.dma_start(
-                scale_rows[0:P:4, :].bitcast(I32), tab_scales.rearrange("a q t -> (a q) t").bitcast(I32)
-            )
-            load_scale_rows(w2_scale_raw, w2_scales)
             nc.sync.dma_start(idx_b[:], offs3)
             nc.sync.dma_start(idx_a[:], offs2)
             bias_b = held([P, 2, PACK], F32, "bias_b")
             nc.sync.dma_start(bias_b[:], bb.rearrange("(b p t) -> p b t", b=2, t=PACK))
+            nc.sync.dma_start(
+                scale_rows[0:P:4, :].bitcast(I32), tab_scales.rearrange("a q t -> (a q) t").bitcast(I32)
+            )
+            load_scale_rows(w2_scale_raw, w2_scales)
+            w2_raw = held([P, 2, 2 * H], U8, "w2_raw")
+            nc.sync.dma_start(w2_raw[:].bitcast(I32), w2_words.rearrange("a p c -> p a c").bitcast(I32))
             table0 = held([P, T], U32, "table0")
             load_table(table0, 0)
             nc.vector.tensor_copy(picked_rows[:], scale_rows[:].indirect(idx[:]))
@@ -103,11 +103,11 @@ def tile_list_burial_kin_scores_kernel(
             )
             return raw
 
+        w1_raw = {}
+        w1_raw[0, 0] = load_rows(w1, 0, slice(0, BANK))
         weight_b = late.tile([P, M], F32, name="weight_b")
         nc.sync.dma_start(weight_b[:], wgb)
-        w1_raw = {}
-        for a in range(2):
-            w1_raw[a, 0] = load_rows(w1, a, slice(0, BANK))
+        w1_raw[1, 0] = load_rows(w1, 1, slice(0, BANK))
         bias_a = late.tile([P, 2, PACK], F32, name="bias_a")
         nc.sync.dma_start(bias_a[:], ba.rearrange("(b p t) -> p b t", b=2, t=PACK))
         weight_a = late.tile([P, M], F32, name="weight_a")
@@ -207,16 +207,16 @@ def tile_list_burial_kin_scores_kernel(
             lo_grouped = extreme(left, right, ALU.min, width)
             return quantize(hi_grouped, "hi" + name, width), quantize(lo_grouped, "lo" + name, width)
 
+        for pair in range(2):
+            round_w1(0, 0, pair, "vector")
         pick_b(0, 0)
-        round_w1(0, 0, 0, "vector")
-        round_w1(0, 0, 1, "scalar")
-        pick_b(0, 1)
         quantize_w1(0, 0)
+        pick_b(0, 1)
+        for pair in range(2):
+            round_w1(1, 0, pair, "scalar")
         pick_b(0, 2)
-        round_w1(1, 0, 0, "scalar")
-        round_w1(1, 0, 1, "scalar")
-        pick_b(0, 3)
         quantize_w1(1, 0)
+        pick_b(0, 3)
 
         w3_raw = [load_rows(w3, a, slice(0, N)) for a in range(2)]
         w4_code = late.tile([P, 2, N], U32, name="w4_code", align_bytes=64)
@@ -235,11 +235,13 @@ def tile_list_burial_kin_scores_kernel(
         for t in range(PACK):
             h = h_slice(w1_operand, bias_a, 0, t)
             nc.vector.tensor_tensor(xa0[:, t, :], h[:].indirect(idx_a[:]), weight_a[:], ALU.mult)
-            round_w1(t // 2, 1, t % 2, "scalar")
-            if t % 2:
-                quantize_w1(t // 2, 1)
 
+        for a in range(2):
+            for pair in range(2):
+                round_w1(a, 1, pair, "scalar")
         hi0, lo0 = extremes(xa0[:], xb[0][:], "0", M)
+        for a in range(2):
+            quantize_w1(a, 1)
         for t in range(PACK):
             pick_b(1, t)
 
@@ -258,13 +260,12 @@ def tile_list_burial_kin_scores_kernel(
             )
 
         first_cols, last_cols = slice(0, FIRST), slice(FIRST, M)
-        ha1, w3_mx = [], []
+        ha1 = []
         xa1 = held([P, PACK, FIRST], F32, "xa1_first", "xa1")
         for t in range(PACK):
             ha1.append(h_slice(w1_operand, bias_a, 1, t))
             pick_part(ha1[t], xa1, t, first_cols)
-            if t % 2:
-                w3_mx.append(round_w3(t // 2))
+        w3_mx = [round_w3(a) for a in range(2)]
         w4_mx = [(w4_code[:, b, :], w4_scale[:, b, :]) for b in range(2)]
 
         def y_pass(y, weight, s, operand, cols, start, stop):

from contextlib import ExitStack

import concourse.mybir as mybir

K, T, S, H, M, N = 1024, 4096, 1024, 1024, 512, 512
FLOPS = 2 * (2 * K * H * S + 2 * H * N * M)

F32 = mybir.dt.float32
BF16 = mybir.dt.bfloat16
I32 = mybir.dt.int32
U32 = mybir.dt.uint32
U16 = mybir.dt.uint16
U8 = mybir.dt.uint8
FP8X4 = mybir.dt.float8_e4m3fn_x4
FP4X4 = mybir.dt.float4_e2m1fn_x4
ALU = mybir.AluOpType
ACT = mybir.ActivationFunctionType

P = 128
PACK = 4
PASS = P * PACK
BANK = 512
LAST = 128
FIRST = M - LAST


def tile_list_burial_kin_scores_kernel(
    tc, tab_words, tab_scales, offs, offs2, offs3, w1, w2_words, w2_scales, ba, bb,
    wga, wgb, w3, w4_words, w4_scales, by, cov, out,
):
    nc = tc.nc
    with ExitStack() as ctx:
        lists = ctx.enter_context(tc.tile_pool(name="lists", bufs=1))
        keep = ctx.enter_context(tc.tile_pool(name="keep", bufs=1))
        ring = ctx.enter_context(tc.tile_pool(name="ring", bufs=4))
        hpool = ctx.enter_context(tc.tile_pool(name="hpool", bufs=6))
        psum = ctx.enter_context(tc.psum_pool(name="psum", bufs=8))

        def held(shape, dtype, name, tag=None):
            return keep.tile(shape, dtype, name=name, tag=tag or name, align_bytes=64)

        idx = lists.tile([P, S // 16], U16, name="idx")
        idx_a = lists.tile([P, M // 16], U16, name="idx_a")
        idx_b = lists.tile([P, M // 16], U16, name="idx_b")

        def load_scale_rows(plane, dram):
            for quad in range(4):
                nc.sync.dma_start(
                    plane[32 * quad : 32 * quad + 4, :, :].bitcast(I32),
                    dram[:, 4 * quad : 4 * quad + 4, :].rearrange("a r c -> r a c").bitcast(I32),
                )

        def load_table(words, a):
            nc.sync.dma_start(
                words[:].bitcast(I32), tab_words[a].rearrange("p t i -> p (t i)").bitcast(I32)
            )

        picked_rows = held([P, S], U8, "picked_rows")
        with tc.tile_pool(name="early", bufs=1) as early:
            scale_rows = early.tile([P, T], U8, name="scale_rows")
            w2_scale_raw = held([P, 2, H], U8, "w2_scale_raw")
            v_scale = [held([P, S], U8, "v_scale%d" % a) for a in range(2)]
            nc.vector.memset(scale_rows[:].bitcast(I32), 0)
            nc.vector.memset(w2_scale_raw[:].bitcast(I32), 0)
            for a in range(2):
                nc.vector.memset(v_scale[a][:].bitcast(I32), 0)

            nc.sync.dma_start(idx[:], offs)
            nc.sync.dma_start(idx_b[:], offs3)
            nc.sync.dma_start(idx_a[:], offs2)
            bias_b = held([P, 2, PACK], F32, "bias_b")
            nc.sync.dma_start(bias_b[:], bb.rearrange("(b p t) -> p b t", b=2, t=PACK))
            nc.sync.dma_start(
                scale_rows[0:P:4, :].bitcast(I32), tab_scales.rearrange("a q t -> (a q) t").bitcast(I32)
            )
            load_scale_rows(w2_scale_raw, w2_scales)
            w2_raw = held([P, 2, 2 * H], U8, "w2_raw")
            nc.sync.dma_start(w2_raw[:].bitcast(I32), w2_words.rearrange("a p c -> p a c").bitcast(I32))
            table0 = held([P, T], U32, "table0")
            load_table(table0, 0)
            nc.vector.tensor_copy(picked_rows[:], scale_rows[:].indirect(idx[:]))

        late = ctx.enter_context(tc.tile_pool(name="late", bufs=1))

        def move_scale_rows(a, quad):
            first = 64 * a + 16 * quad
            nc.sync.dma_start(
                v_scale[a][32 * quad : 32 * quad + 4, :].bitcast(I32),
                picked_rows[first : first + 16 : 4, :].bitcast(I32),
            )

        for k in range(4):
            move_scale_rows(k // 4, k % 4)
        table1 = late.tile([P, T], U32, name="table1")
        load_table(table1, 1)
        for k in range(4, 8):
            move_scale_rows(k // 4, k % 4)

        def load_rows(dram, a, cols):
            raw = late.tile([P, PACK, BANK], F32, name="raw", bufs=4)
            nc.sync.dma_start(
                raw[:], dram[PASS * a : PASS * (a + 1), cols].rearrange("(p j) c -> p j c", j=PACK)
            )
            return raw

        w1_raw = {}
        w1_raw[0, 0] = load_rows(w1, 0, slice(0, BANK))
        weight_b = late.tile([P, M], F32, name="weight_b")
        nc.sync.dma_start(weight_b[:], wgb)
        w1_raw[1, 0] = load_rows(w1, 1, slice(0, BANK))
        bias_a = late.tile([P, 2, PACK], F32, name="bias_a")
        nc.sync.dma_start(bias_a[:], ba.rearrange("(b p t) -> p b t", b=2, t=PACK))
        weight_a = late.tile([P, M], F32, name="weight_a")
        nc.sync.dma_start(weight_a[:], wga)
        for a in range(2):
            w1_raw[a, 1] = load_rows(w1, a, slice(BANK, 2 * BANK))

        w2_code = late.tile([P, 2 * 2 * H], U8, name="w2_code", align_bytes=64)
        nc.vector.tensor_copy(
            w2_code[:].bitcast(U16).rearrange("p (g t m) -> p g t m", t=PACK, m=P),
            w2_raw[:].rearrange("p a c -> p (a c)").bitcast(U16).rearrange("p (g m t) -> p g t m", t=PACK, m=P),
        )
        v_code0 = late.tile([P, S], U32, name="v_code0", align_bytes=64)
        nc.vector.tensor_copy(v_code0[:], table0[:].indirect(idx[:]))
        v_code = {(0, half): v_code0[:, BANK * half : BANK * (half + 1)] for half in range(2)}
        w2_scale = held([P, 2 * H], U8, "w2_scale")
        nc.vector.tensor_copy(
            w2_scale[:].rearrange("p (g t m) -> p g t m", t=PACK, m=P),
            w2_scale_raw[:].rearrange("p a (b m t) -> p (a b) t m", t=PACK, m=P),
        )
        for half in range(2):
            picked = held([P, BANK], U32, "v_code1%d" % half, None if half else "w2_scale_raw")
            nc.vector.tensor_copy(picked[:], table1[:].indirect(idx[:, 32 * half : 32 * (half + 1)]))
            v_code[1, half] = picked[:]

        def copy_on(engine, dst, src):
            if engine == "scalar":
                nc.scalar.copy(dst, src)
            else:
                nc.vector.tensor_copy(dst, src)

        def quantize(grouped, name, width=BANK):
            code = held([P, width], U32, name + "_code")
            scale = held([P, width], U8, name + "_scale")
            nc.vector.quantize_mx(out=code[:].bitcast(FP8X4), scales=scale[:], in_=grouped[:])
            return code, scale

        w1_grouped = {}
        w1_mx = {}

        def round_w1(a, b, pair, engine):
            if (a, b) not in w1_grouped:
                w1_grouped[a, b] = ring.tile([P, PACK * BANK], BF16, name="grouped", align_bytes=64)
            ts = slice(2 * pair, 2 * pair + 2)
            copy_on(
                engine,
                w1_grouped[a, b][:].rearrange("p (t m j) -> p m j t", t=PACK, j=PACK)[:, :, :, ts],
                w1_raw[a, b][:].rearrange("p j (m t) -> p m j t", t=PACK)[:, :, :, ts],
            )

        def quantize_w1(a, b):
            w1_mx[a, b] = quantize(w1_grouped[a, b], "w1_%d%d" % (a, b))

        def w1_operand(a, b, t):
            code, scale = w1_mx[a, b]
            return code[:, P * t : P * (t + 1)].bitcast(FP8X4), scale[:, P * t : P * (t + 1)]

        def w2_operand(a, b, t):
            col = H * a + BANK * b + P * t
            return w2_code[:, 2 * col : 2 * (col + P)].bitcast(FP4X4), w2_scale[:, col : col + P]

        def h_slice(operand, bias, b, t):
            h = hpool.tile([P, S], F32, name="h")
            for half in range(2):
                cols = slice(BANK * half, BANK * (half + 1))
                acc = psum.tile([P, BANK], F32, name="acc")
                for a in range(2):
                    code, scale = operand(a, b, t)
                    nc.tensor.matmul_mx(
                        out=acc[:], lhsT=code, lhsT_scale=scale,
                        rhs=v_code[a, half].bitcast(FP8X4), rhs_scale=v_scale[a][:, cols],
                        start=(a == 0), stop=(a == 1),
                    )
                nc.scalar.activation(h[:, cols], acc[:], ACT.Identity, bias=bias[:, b, t : t + 1])
            return h

        xa0 = held([P, PACK, M], F32, "xa0")
        xb = [held([P, PACK, M], F32, "xb%d" % b) for b in range(2)]


        def pick_b(b, t):
            h = h_slice(w2_operand, bias_b, b, t)
            nc.vector.tensor_tensor(xb[b][:, t, :], h[:].indirect(idx_b[:]), weight_b[:], ALU.mult)

        def extreme(left, right, op, width):
            grouped = ring.tile([P, PACK * width], BF16, name="grouped", align_bytes=64)
            nc.vector.tensor_tensor(
                grouped[:].rearrange("p (c i t) -> p c t i", i=2, t=PACK),
                left.rearrange("p t (c i) -> p c t i", i=2),
                right.rearrange("p t (c i) -> p c t i", i=2),
                op,
            )
            return grouped

        def extremes(left, right, name, width):
            hi_grouped = extreme(left, right, ALU.max, width)
            lo_grouped = extreme(left, right, ALU.min, width)
            return quantize(hi_grouped, "hi" + name, width), quantize(lo_grouped, "lo" + name, width)

        for pair in range(2):
            round_w1(0, 0, pair, "vector")
        pick_b(0, 0)
        quantize_w1(0, 0)
        pick_b(0, 1)
        for pair in range(2):
            round_w1(1, 0, pair, "scalar")
        pick_b(0, 2)
        quantize_w1(1, 0)
        pick_b(0, 3)

        w3_raw = [load_rows(w3, a, slice(0, N)) for a in range(2)]
        w4_code = late.tile([P, 2, N], U32, name="w4_code", align_bytes=64)
        w4_scale = late.tile([P, 2, N], U8, name="w4_scale", align_bytes=64)
        nc.vector.memset(w4_scale[:].bitcast(I32), 0)
        nc.sync.dma_start(
            w4_code[:].bitcast(I32), w4_words.rearrange("a p c i -> p a (c i)").bitcast(I32)
        )
        load_scale_rows(w4_scale, w4_scales)
        bias_y = late.tile([P, N // P], F32, name="bias_y")
        with nc.allow_non_contiguous_dma(reason="one bias value for each output row"):
            nc.sync.dma_start(bias_y[:], by.rearrange("(s p) -> p s", p=P))
        cover = late.tile([P, M], F32, name="cover")
        nc.sync.dma_start(cover[:], cov.partition_broadcast(P))

        for t in range(PACK):
            h = h_slice(w1_operand, bias_a, 0, t)
            nc.vector.tensor_tensor(xa0[:, t, :], h[:].indirect(idx_a[:]), weight_a[:], ALU.mult)

        for a in range(2):
            for pair in range(2):
                round_w1(a, 1, pair, "scalar")
        hi0, lo0 = extremes(xa0[:], xb[0][:], "0", M)
        for a in range(2):
            quantize_w1(a, 1)
        for t in range(PACK):
            pick_b(1, t)

        def round_w3(a):
            grouped = ring.tile([P, PACK * BANK], BF16, name="grouped", align_bytes=64)
            nc.scalar.copy(
                grouped[:].rearrange("p (c i j) -> p c j i", i=2, j=PACK),
                w3_raw[a][:].rearrange("p j (c i) -> p c j i", i=2),
            )
            return quantize(grouped, "w3_%d" % a)

        def pick_part(h, xa1, t, cols):
            nc.vector.tensor_tensor(
                xa1[:, t, :], h[:].indirect(idx_a[:, cols.start // 16 : cols.stop // 16]),
                weight_a[:, cols], ALU.mult,
            )

        first_cols, last_cols = slice(0, FIRST), slice(FIRST, M)
        ha1 = []
        xa1 = held([P, PACK, FIRST], F32, "xa1_first", "xa1")
        for t in range(PACK):
            ha1.append(h_slice(w1_operand, bias_a, 1, t))
            pick_part(ha1[t], xa1, t, first_cols)
        w3_mx = [round_w3(a) for a in range(2)]
        w4_mx = [(w4_code[:, b, :], w4_scale[:, b, :]) for b in range(2)]

        def y_pass(y, weight, s, operand, cols, start, stop):
            rows = slice(P * s, P * (s + 1))
            nc.tensor.matmul_mx(
                out=y, lhsT=weight[0][:, rows].bitcast(FP8X4), lhsT_scale=weight[1][:, rows],
                rhs=operand[0][:, cols].bitcast(FP8X4), rhs_scale=operand[1][:, cols],
                start=start, stop=stop,
            )

        hi1, lo1 = extremes(xa1[:], xb[1][:, :, first_cols], "1_first", FIRST)
        y_first = [psum.tile([P, FIRST], F32, name="y_first%d" % s, tag="acc") for s in range(N // P)]
        products = [(w3_mx[0], hi0), (w4_mx[0], lo0), (w3_mx[1], hi1), (w4_mx[1], lo1)]
        for k, (weight, operand) in enumerate(products):
            for s in range(N // P):
                for cols in (slice(0, 256), slice(256, FIRST)):
                    y_pass(
                        y_first[s][:, cols], weight, s, operand, cols,
                        k == 0 and cols.start == 0, k == 3 and cols.stop == FIRST,
                    )
        bounded_first = held([P, N // P, FIRST], F32, "bounded_first")
        for s in range(N // P):
            nc.scalar.activation(bounded_first[:, s, :], y_first[s][:], ACT.Tanh, bias=bias_y[:, s : s + 1])

        xa1 = held([P, PACK, LAST], F32, "xa1_last", "xa1")
        for t in range(PACK):
            pick_part(ha1[t], xa1, t, last_cols)
        hi1, lo1 = extremes(xa1[:], xb[1][:, :, last_cols], "1_last", LAST)
        y_last = psum.tile([P, N // P, LAST], F32, name="y_last", tag="acc")
        products = [
            (w3_mx[0], hi0, last_cols), (w4_mx[0], lo0, last_cols),
            (w3_mx[1], hi1, slice(0, LAST)), (w4_mx[1], lo1, slice(0, LAST)),
        ]
        for k, (weight, operand, cols) in enumerate(products):
            for s in range(N // P):
                y_pass(y_last[:, s, :], weight, s, operand, cols, k == 0 and s == 0, k == 3 and s == 3)
        bounded_last = held([P, N // P, LAST], F32, "bounded_last")
        for s in range(N // P):
            nc.scalar.activation(bounded_last[:, s, :], y_last[:, s, :], ACT.Tanh, bias=bias_y[:, s : s + 1])

        def store_scores(bounded, s0, count, cols, name):
            width = cols.stop - cols.start
            score = held([P, count, width], F32, name)
            nc.vector.tensor_tensor(
                score[:], bounded[:, s0 : s0 + count, :],
                cover[:, cols].unsqueeze(1).to_broadcast([P, count, width]), ALU.mult,
            )
            nc.sync.dma_start(
                out[P * s0 : P * (s0 + count), cols].rearrange("(k p) m -> p k m", p=P), score[:]
            )

        for pair in range(2):
            store_scores(bounded_first, 2 * pair, 2, first_cols, "score_first%d" % pair)
        store_scores(bounded_last, 0, N // P, last_cols, "score_last")
